import numpy as np
import ml_dtypes


def mxq(x, axis, fmt="e4m3"):
    dtype, down = {"e4m3": (ml_dtypes.float8_e4m3fn, 7), "e5m2": (ml_dtypes.float8_e5m2, 14)}[fmt]
    v = np.moveaxis(np.asarray(x, np.float32).astype(ml_dtypes.bfloat16).astype(np.float64), axis, -1)
    blocks = v.reshape(v.shape[:-1] + (-1, 32))
    amax = np.abs(blocks).max(-1, keepdims=True)
    byte = np.maximum(np.where(amax > 0, np.frexp(amax)[1] - 1 + 127, 0) - down, 1)
    scale = np.exp2(byte - 127.0)
    codes = (blocks / scale).astype(np.float32).astype(dtype).astype(np.float64)
    return np.moveaxis((codes * scale).reshape(v.shape), -1, axis)


WIDE = False


def mx_kscale(k):
    if not WIDE:
        return np.ones(k)
    levels = np.array([10, -10, 5, -5, 0])
    if k % 512:
        return np.exp2(np.random.permutation(np.resize(levels, k // 32))).repeat(32)
    a = np.empty((k // 512, 16))
    for p in range(k // 512):
        a[p, :8] = np.random.permutation(np.resize(levels, 8))
        for g in range(8):
            far = levels[np.abs(levels - a[p, g]) >= 10]
            a[p, g + 8] = far[np.random.randint(len(far))]
    return np.exp2(a.ravel()).repeat(32)


BF16 = ml_dtypes.bfloat16


def bf(x):
    return np.asarray(x, np.float32).astype(BF16)


def f64(x):
    return np.asarray(x).astype(np.float64)


E2M1 = np.array([0.0, 0.5, 1.0, 1.5, 2.0, 3.0, 4.0, 6.0, -0.0, -0.5, -1.0, -1.5, -2.0, -3.0, -4.0, -6.0])


def pack_weight(w, fmt):
    k, n = w.shape
    w = f64(bf(w)).reshape(k // 32, 32, n)
    amax = np.abs(w).max(1)
    if fmt == "e4m3":
        byte = np.frexp(amax)[1] - 1 + 127 - 7
    else:
        mant, ex = np.frexp(amax / 6.0)
        byte = np.where(mant > 0.5, ex, ex - 1) + 127
    byte = np.clip(np.where(amax > 0, byte, 1), 1, 254)
    scaled = (w * np.exp2(127.0 - byte)[:, None, :]).reshape(k, n).astype(np.float32)
    by_word = np.ascontiguousarray(scaled.reshape(k // 512, 128, 4, n).transpose(0, 1, 3, 2))
    if fmt == "e4m3":
        words = by_word.astype(ml_dtypes.float8_e4m3fn).view(np.uint8)
    else:
        c = by_word.astype(ml_dtypes.float4_e2m1fn).view(np.uint8) & 0xF
        words = c[..., 0::2] | (c[..., 1::2] << 4)
    return np.ascontiguousarray(words), np.ascontiguousarray(byte.astype(np.uint8).reshape(k // 512, 16, n))


def unpack_weight(words, scales, fmt):
    g, p, n, _ = words.shape
    if fmt == "e4m3":
        vals = np.ascontiguousarray(words).view(ml_dtypes.float8_e4m3fn).astype(np.float64)
    else:
        nib = np.empty((g, p, n, 4), np.uint8)
        nib[..., 0::2] = words & 0xF
        nib[..., 1::2] = words >> 4
        vals = E2M1[nib]
    vals = vals * np.repeat(np.exp2(scales.astype(np.float64) - 127.0), 8, axis=1)[..., None]
    return vals.transpose(0, 1, 3, 2).reshape(g * 512, n)
def pack4(w):
    words, scales = pack_weight(w, "e2m1")
    return words.reshape(words.shape[0], 128, -1), scales


def unpack4(words, scales):
    return unpack_weight(words.reshape(words.shape[0], 128, -1, 2), scales, "e2m1")


T, D, DS, F = 1024, 1024, 1024, 1024


def sigmoid(v):
    return 1.0 / (1.0 + np.exp(-v))


def draw0():
    s, r, t = mx_kscale(D), mx_kscale(DS), mx_kscale(F)
    k_recv = bf(np.random.standard_normal((T, D)) * s)
    k_share = bf(np.random.standard_normal((T, DS)) * r)
    w_recv_words, w_recv_scales = pack4(np.random.standard_normal((D, F)) / np.sqrt(D) / s[:, None])
    w_share_words, w_share_scales = pack4(np.random.standard_normal((DS, F)) / np.sqrt(DS) / r[:, None])
    g_hid = bf((1.0 + 0.1 * np.random.standard_normal(F)) * t)
    w_delta_words, w_delta_scales = pack4(np.random.standard_normal((F, D)) * 2.0 / np.sqrt(F) / t[:, None] * s)
    w_gate_words, w_gate_scales = pack4(np.random.standard_normal((F, D)) * 1.5 / np.sqrt(F) / t[:, None])
    return {
        "k_recv": k_recv,
        "k_share": k_share,
        "w_recv_words": w_recv_words,
        "w_recv_scales": w_recv_scales,
        "w_share_words": w_share_words,
        "w_share_scales": w_share_scales,
        "g_hid": g_hid,
        "w_delta_words": w_delta_words,
        "w_delta_scales": w_delta_scales,
        "w_gate_words": w_gate_words,
        "w_gate_scales": w_gate_scales,
    }


def core(k_recv, k_share, w_recv_words, w_recv_scales, w_share_words, w_share_scales, g_hid, w_delta_words, w_delta_scales, w_gate_words, w_gate_scales):
    kr = f64(k_recv)
    u = (mxq(kr, 1, "e4m3") @ unpack4(w_recv_words, w_recv_scales)) + (mxq(f64(k_share), 1, "e4m3") @ unpack4(w_share_words, w_share_scales))
    h = u * sigmoid(u) * f64(g_hid)[None, :]
    hq = mxq(h, 1, "e4m3")
    delta = hq @ unpack4(w_delta_words, w_delta_scales)
    gate = sigmoid(hq @ unpack4(w_gate_words, w_gate_scales))
    return kr + gate * delta


def e4m3fn_bytes(y):
    return np.clip(np.asarray(y, np.float64), -448.0, 448.0).astype(np.float32).astype(ml_dtypes.float8_e4m3fn).view(np.uint8)


def e4m3fn_values(b):
    return np.asarray(b, np.uint8).view(ml_dtypes.float8_e4m3fn).astype(np.float64)


def setup_inputs():
    d = draw0()
    x0 = np.asarray(d['k_share']).astype(np.float64)
    s = (np.max(np.abs(x0), axis=(0,), keepdims=True) / 448.0).astype(np.float32)
    out = {}
    for k, v in d.items():
        if k == 'k_share':
            out['k_share_bytes'] = e4m3fn_bytes(x0 / s.astype(np.float64))
            out['k_share_scale'] = s
        else:
            out[k] = v
    return out


def reference(k_recv, k_share_bytes, k_share_scale, w_recv_words, w_recv_scales, w_share_words, w_share_scales, g_hid, w_delta_words, w_delta_scales, w_gate_words, w_gate_scales):
    return core(k_recv, e4m3fn_values(k_share_bytes) * k_share_scale.astype(np.float64), w_recv_words, w_recv_scales, w_share_words, w_share_scales, g_hid, w_delta_words, w_delta_scales, w_gate_words, w_gate_scales)

@@ -1,0 +1,427 @@
+from contextlib import ExitStack
+
+import concourse.mybir as mybir
+from concourse.masks import make_identity
+
+T, D, F = 1024, 1024, 1024
+FLOPS = 4 * 2 * T * D * F
+
+F32 = mybir.dt.float32
+BF16 = mybir.dt.bfloat16
+U32 = mybir.dt.uint32
+I32 = mybir.dt.int32
+U8 = mybir.dt.uint8
+FP8 = mybir.dt.float8_e4m3fn
+FP8X4 = mybir.dt.float8_e4m3fn_x4
+FP4X4 = mybir.dt.float4_e2m1fn_x4
+ACT = mybir.ActivationFunctionType
+ALU = mybir.AluOpType
+
+P = 128
+CFG = dict(ld1=0, tr1=1, cv1=False, shr=True, shs=False, sh1=True, late1=0, castpos=0, addpos=0, shpos=2, gd=0)
+HALF = 512
+TILES = T // P
+PASSES = D // 512
+
+
+def tile_cachetocachegatedkeyfuser_w4_kernel(
+    tc, k_recv, k_share_bytes, k_share_scale, w_recv_words, w_recv_scales, w_share_words, w_share_scales,
+    g_hid, w_delta_words, w_delta_scales, w_gate_words, w_gate_scales, out,
+):
+    nc = tc.nc
+    with ExitStack() as ctx:
+        keep = ctx.enter_context(tc.tile_pool(name="keep", bufs=1))
+        inp = ctx.enter_context(tc.tile_pool(name="inp", bufs=TILES))
+        work = ctx.enter_context(tc.tile_pool(name="work", bufs=3))
+        psum = ctx.enter_context(tc.psum_pool(name="psum", bufs=2))
+        ctx.enter_context(tc.manual_schedule())
+
+        ident = keep.tile([P, P], F32, name="ident", align_bytes=64)
+        make_identity(nc, ident[:])
+        warm = keep.tile([P, 1], F32, name="warm")
+        nc.vector.memset(warm[:], 0.0)
+        nc.scalar.activation(out=warm[:], in_=warm[:], func=ACT.Silu)
+
+        words = {}
+        scales = {}
+        for nm in ("recv", "share", "gate", "delta"):
+            wt = keep.tile([P, PASSES, 2 * F], U8, name="words_" + nm, align_bytes=256)
+            st = keep.tile([P, PASSES, F], U8, name="scales_" + nm, align_bytes=256)
+            nc.vector.memset(st[:].rearrange("p g n -> p (g n)").bitcast(I32), 0)
+            words[nm] = wt
+            scales[nm] = st
+
+        kr_in = {}
+        ks_in = {}
+
+        def load_recv(i):
+            kr_in[i] = inp.tile([P, D], BF16, name="kr", align_bytes=64)
+            nc.sync.dma_start(out=kr_in[i][:], in_=k_recv[i * P : (i + 1) * P, :])
+
+        def load_share(i):
+            ks_in[i] = inp.tile([P, D], U8, name="kb", align_bytes=64)
+            nc.sync.dma_start(out=ks_in[i][:], in_=k_share_bytes[i * P : (i + 1) * P, :])
+
+        def load_words(nm, w_words):
+            nc.sync.dma_start(
+                out=words[nm][:].bitcast(I32), in_=w_words.bitcast(I32).rearrange("g p n -> p g n")
+            )
+
+        def load_scales(nm, w_scales):
+            sc = w_scales.bitcast(I32).rearrange("g q n -> q g n")
+            for q in range(4):
+                nc.sync.dma_start(
+                    out=scales[nm][32 * q : 32 * q + 4, :, :].bitcast(I32), in_=sc[4 * q : 4 * q + 4, :, :]
+                )
+
+        kscale = keep.tile([P, 4 * PASSES], F32, name="kscale")
+        gcol = keep.tile([P, 8], BF16, name="gcol")
+
+        def load_kscale():
+            nc.sync.dma_start(
+                out=kscale[:].rearrange("p (g t) -> p g t", t=4),
+                in_=k_share_scale.rearrange("o (g p t) -> p (o g) t", p=P, t=4),
+            )
+
+        def load_gain():
+            nc.sync.dma_start(out=gcol[:], in_=g_hid.rearrange("(n m) -> n m", m=8))
+
+        load_share(0)
+        load_recv(0)
+        load_kscale()
+        load_scales("recv", w_recv_scales)
+        load_words("recv", w_recv_words)
+        if CFG["ld1"] == 0:
+            load_recv(1)
+            load_share(1)
+        load_words("share", w_share_words)
+        load_scales("share", w_share_scales)
+        if CFG["ld1"] == 1:
+            load_recv(1)
+            load_share(1)
+        load_gain()
+        for i in (2, 3):
+            load_recv(i)
+            load_share(i)
+        load_words("gate", w_gate_words)
+        load_scales("gate", w_gate_scales)
+        load_recv(4)
+        load_share(4)
+        load_words("delta", w_delta_words)
+        load_scales("delta", w_delta_scales)
+        for i in range(5, TILES):
+            load_recv(i)
+            load_share(i)
+        ksb = {}
+        krs = {}
+        kss = {}
+        trp = {}
+        xg = {}
+        xc = {}
+        up = {}
+        hs = {}
+        hg = {}
+        hc = {}
+        gd = {}
+        th = {}
+        prd = {}
+        res = {}
+
+        def cast_share(i):
+            t = work.tile([P, D], BF16, name="ksb", align_bytes=64)
+            nc.scalar.copy(out=t[:], in_=ks_in[i][:].bitcast(FP8))
+            ksb[i] = t
+
+        def shuffle_recv(i):
+            t = work.tile([P, D], BF16, name="krs", align_bytes=64)
+            nc.scalar.copy(
+                out=t[:].bitcast(F32).rearrange("p (u x) -> p u x", u=2),
+                in_=kr_in[i][:].bitcast(F32).rearrange("p (x u) -> p u x", u=2),
+            )
+            krs[i] = t
+
+        def shuffle_share(i):
+            t = work.tile([P, D], BF16, name="kss", align_bytes=64)
+            nc.scalar.copy(
+                out=t[:].bitcast(F32).rearrange("p (u x) -> p u x", u=2),
+                in_=ksb[i][:].bitcast(F32).rearrange("p (x u) -> p u x", u=2),
+            )
+            kss[i] = t
+
+        def transpose_recv(i):
+            if i in krs:
+                transpose_words(krs[i], True, ("r", i))
+            else:
+                transpose_words(kr_in[i], False, ("r", i))
+
+        def transpose_share(i):
+            if i in kss:
+                transpose_words(kss[i], True, ("s", i))
+            else:
+                transpose_words(ksb[i], False, ("s", i))
+
+        def transpose_words(src, shuffled, key):
+            bank = psum.tile([P, 4, P], F32, name="tr", bufs=3)
+            w = src[:].bitcast(F32)
+            for g in range(PASSES):
+                for u in range(2):
+                    if shuffled:
+                        blk = w[:, (2 * u + g) * P : (2 * u + g + 1) * P]
+                    else:
+                        blk = w[:, 256 * g + u : 256 * (g + 1) : 2]
+                    nc.tensor.transpose(bank[:, 2 * u + g, :], blk, ident[:])
+            trp[key] = bank
+
+        def copy_out(eng_copy, bank, dst):
+            eng_copy(
+                out=dst.bitcast(F32).rearrange("p (x u) -> p x u", u=2),
+                in_=bank[:].rearrange("p (u g) r -> p (g r) u", u=2),
+            )
+
+        def new_xg(i):
+            xg[i] = work.tile([P, 2 * D], BF16, name="xg", align_bytes=64)
+
+        def copy_recv(i, on_vector=False):
+            copy_out(nc.vector.tensor_copy if on_vector else nc.scalar.copy, trp["r", i], xg[i][:, 0:D])
+
+        def scale_share(i):
+            v = trp["s", i][:].rearrange("p a r -> p (a r)").bitcast(BF16)
+            v = v.rearrange("p (u g r e) -> p g r u e", g=2, u=2, e=2)
+            o = xg[i][:, D : 2 * D].rearrange("p (g r u e) -> p g r u e", g=2, u=2, e=2)
+            s = kscale[:].rearrange("p (g u e) -> p g u e", u=2, e=2)
+            nc.vector.tensor_tensor(
+                out=o, in0=v, in1=s.unsqueeze(2).to_broadcast([P, PASSES, P, 2, 2]), op=ALU.mult
+            )
+
+        def new_xc(i):
+            c = work.tile([P, 512], U32, name="xc", align_bytes=64)
+            s = work.tile([P, 512], U8, name="xs", align_bytes=64)
+            xc[i] = (c, s)
+
+        def quant_x(i, a, b):
+            c, s = xc[i]
+            nc.vector.quantize_mx(
+                out=c[:, 256 * a : 256 * b].bitcast(FP8X4), scales=s[:, 256 * a : 256 * b], in_=xg[i][:, D * a : D * b]
+            )
+
+        def new_up(i):
+            for h in range(2):
+                up[i, h] = psum.tile([P, HALF], F32, name="up", bufs=2)
+
+        def mm_up(i, h, srcs):
+            c, s = xc[i]
+            for si in srcs:
+                nm = ("recv", "share")[si]
+                for g in range(PASSES):
+                    col = slice(256 * si + P * g, 256 * si + P * (g + 1))
+                    nc.tensor.matmul_mx(
+                        out=up[i, h][:],
+                        lhsT=c[:, col].bitcast(FP8X4),
+                        lhsT_scale=s[:, col],
+                        rhs=words[nm][:, g, 2 * HALF * h : 2 * HALF * (h + 1)].bitcast(FP4X4),
+                        rhs_scale=scales[nm][:, g, HALF * h : HALF * (h + 1)],
+                        start=(si == 0 and g == 0),
+                        stop=(si == 1 and g == PASSES - 1),
+                    )
+
+        sl = {}
+
+        def silu(i, h):
+            if h == 0:
+                sl[i] = work.tile([P, F], F32, name="sl", bufs=3, align_bytes=64)
+            nc.scalar.activation(
+                out=sl[i][:].rearrange("p (u g m e) -> p g u m e", u=2, g=2, e=2)[:, h],
+                in_=up[i, h][:].rearrange("p (m u e) -> p u m e", u=2, e=2),
+                func=ACT.Silu,
+            )
+
+        def gain(i):
+            hs[i] = work.tile([P, F], BF16, name="hs", bufs=4, align_bytes=64)
+            nc.vector.tensor_tensor(out=hs[i][:], in0=sl[i][:], in1=gfull[:], op=ALU.mult)
+
+        def copy_h(i):
+            hg[i] = work.tile([P, F], BF16, name="hg", align_bytes=64)
+            copy_out(nc.scalar.copy, trp["h", i], hg[i][:])
+
+        def quant_h(i):
+            c = work.tile([P, 256], U32, name="hc", align_bytes=64)
+            s = work.tile([P, 256], U8, name="hsc", align_bytes=64)
+            nc.vector.quantize_mx(out=c[:].bitcast(FP8X4), scales=s[:], in_=hg[i][:])
+            hc[i] = (c, s)
+
+        def mm_out(i, nm, h):
+            if i == TILES - 1 and nm == "gate":
+                bank = psum.tile([P, HALF], F32, name="up", bufs=2)
+            else:
+                bank = psum.tile([P, HALF], F32, name="gd", bufs=3)
+            c, s = hc[i]
+            for g in range(PASSES):
+                col = slice(P * g, P * (g + 1))
+                nc.tensor.matmul_mx(
+                    out=bank[:],
+                    lhsT=c[:, col].bitcast(FP8X4),
+                    lhsT_scale=s[:, col],
+                    rhs=words[nm][:, g, 2 * HALF * h : 2 * HALF * (h + 1)].bitcast(FP4X4),
+                    rhs_scale=scales[nm][:, g, HALF * h : HALF * (h + 1)],
+                    start=(g == 0),
+                    stop=(g == PASSES - 1),
+                )
+            gd[i, nm, h] = bank
+
+        def tanh(i, h):
+            t = work.tile([P, HALF], F32, name="th", align_bytes=64)
+            nc.scalar.activation(out=t[:], in_=gd[i, "gate", h][:], func=ACT.Tanh, scale=0.5)
+            th[i, h] = t
+
+        def gate_delta(i, h):
+            if h == 0:
+                prd[i] = work.tile([P, D], F32, name="prd", bufs=3, align_bytes=64)
+            nc.vector.scalar_tensor_tensor(
+                out=prd[i][:, HALF * h : HALF * (h + 1)], in0=th[i, h][:], scalar=1.0, in1=gd[i, "delta", h][:], op0=ALU.add, op1=ALU.mult
+            )
+
+        def add_store(i, c0=0, c1=D):
+            if c0 == 0:
+                res[i] = work.tile([P, D], F32, name="res", bufs=3, align_bytes=64)
+            nc.vector.scalar_tensor_tensor(
+                out=res[i][:, c0:c1], in0=prd[i][:, c0:c1], scalar=0.5, in1=kr_in[i][:, c0:c1],
+                op0=ALU.mult, op1=ALU.add,
+            )
+            nc.sync.dma_start(out=out[i * P : (i + 1) * P, c0:c1], in_=res[i][:, c0:c1])
+
+        gfull = keep.tile([P, F], BF16, name="gfull", align_bytes=64)
+
+        def spread_gain():
+            gw = gcol[:].bitcast(F32)
+            gbank = psum.tile([P, 4, P], F32, name="tr", bufs=3)
+            for m in range(4):
+                nc.tensor.transpose(gbank[:, m, :], gw[:, m : m + 1].to_broadcast([P, P]), ident[:])
+            for g in range(PASSES):
+                nc.vector.tensor_copy(
+                    out=gfull[:].bitcast(F32).rearrange("p (u g n a) -> p g u n a", u=2, g=2, a=2)[:, g],
+                    in_=gbank[:, :, 64 * g : 64 * (g + 1)].rearrange("p (a u) n -> p u n a", u=2),
+                )
+
+        cast_share(0)
+        transpose_recv(0)
+        transpose_share(0)
+        new_xg(0)
+        new_xc(0)
+        new_xg(1)
+        new_xc(1)
+        copy_recv(0, on_vector=True)
+        quant_x(0, 0, 1)
+        scale_share(0)
+        quant_x(0, 1, 2)
+        new_up(0)
+        if CFG["shr"] and CFG["sh1"]:
+            shuffle_recv(1)
+        cast_share(1)
+        if CFG["shs"] and CFG["sh1"]:
+            shuffle_share(1)
+        if CFG["tr1"] == 0:
+            transpose_recv(1)
+            transpose_share(1)
+        mm_up(0, 0, (0,))
+        mm_up(0, 1, (0,))
+        if CFG["tr1"] == 1:
+            transpose_recv(1)
+            transpose_share(1)
+        copy_recv(1, on_vector=CFG["cv1"])
+        scale_share(1)
+        quant_x(1, 0, 2)
+        mm_up(0, 0, (1,))
+        mm_up(0, 1, (1,))
+        if CFG["shr"]:
+            shuffle_recv(2)
+        cast_share(2)
+        if CFG["shs"]:
+            shuffle_share(2)
+        spread_gain()
+        silu(0, 0)
+        silu(0, 1)
+        gain(0)
+        for i in range(1, TILES + 1):
+            hs_now = [i - 2] if 2 <= i < TILES else []
+            if i == TILES - 1:
+                hs_now = [i - 2, i - 1]
+            if i == TILES:
+                hs_now = [TILES - 1]
+            xn = i + 1 if i + 1 < TILES else None
+            xs = i + 2 if i + 2 < TILES else None
+            for j in hs_now:
+                transpose_words(hs[j], True, ("h", j))
+            if xn is not None:
+                transpose_recv(xn)
+                transpose_share(xn)
+                new_xg(xn)
+                new_xc(xn)
+            if i == 1 and CFG["late1"]:
+                pass
+            for j in hs_now:
+                copy_h(j)
+            if xn is not None:
+                copy_recv(xn)
+            for j in hs_now:
+                quant_h(j)
+            if xs is not None and CFG["castpos"] == 0:
+                cast_share(xs)
+            if CFG["shr"] and xs is not None and CFG["shpos"] == 2:
+                shuffle_recv(xs)
+            if CFG["shs"] and xs is not None and CFG["shpos"] == 2:
+                shuffle_share(xs)
+            if xn is not None:
+                scale_share(xn)
+                quant_x(xn, 0, 2)
+            if i < TILES:
+                new_up(i)
+                mm_up(i, 0, (0, 1))
+                silu(i, 0)
+                if i >= 3 and CFG["addpos"] == 0:
+                    add_store(i - 3)
+                mm_up(i, 1, (0, 1))
+                if xs is not None and CFG["castpos"] == 1:
+                    cast_share(xs)
+                if CFG["shr"] and xs is not None and CFG["shpos"] == 3:
+                    shuffle_recv(xs)
+                if CFG["shs"] and xs is not None and CFG["shpos"] == 3:
+                    shuffle_share(xs)
+                silu(i, 1)
+                if i >= 3 and CFG["addpos"] == 1:
+                    add_store(i - 3)
+                gain(i)
+            last = [i - 2] if 2 <= i < TILES else ([TILES - 2, TILES - 1] if i == TILES else [])
+            if CFG["shr"] and xs is not None and CFG["shpos"] == 0:
+                shuffle_recv(xs)
+            if CFG["shs"] and xs is not None and CFG["shpos"] == 0:
+                shuffle_share(xs)
+            for j in last:
+                if i == TILES and j == TILES - 2:
+                    add_store(j - 1)
+                if CFG["gd"] == 0 or j == TILES - 1:
+                    mm_out(j, "gate", 0)
+                    tanh(j, 0)
+                    mm_out(j, "delta", 0)
+                    if j == TILES - 1:
+                        add_store(j - 1)
+                    gate_delta(j, 0)
+                    if j == TILES - 1:
+                        add_store(j, 0, HALF)
+                    mm_out(j, "gate", 1)
+                    tanh(j, 1)
+                    mm_out(j, "delta", 1)
+                    gate_delta(j, 1)
+                else:
+                    mm_out(j, "gate", 0)
+                    tanh(j, 0)
+                    mm_out(j, "gate", 1)
+                    tanh(j, 1)
+                    mm_out(j, "delta", 0)
+                    gate_delta(j, 0)
+                    mm_out(j, "delta", 1)
+                    gate_delta(j, 1)
+            if CFG["shr"] and xs is not None and CFG["shpos"] == 1:
+                shuffle_recv(xs)
+            if CFG["shs"] and xs is not None and CFG["shpos"] == 1:
+                shuffle_share(xs)
+        add_store(TILES - 1, HALF, D)

@@ -18,7 +18,7 @@ ACT = mybir.ActivationFunctionType
 ALU = mybir.AluOpType
 
 P = 128
-CFG = dict(ld1=0, tr1=1, cv1=False, shr=True, shs=False, sh1=True, late1=0, castpos=0, addpos=0, shpos=2, gd=0)
+CFG = dict(cu=3, ks0=2, castv=3, sh2e=False, ld1=0, tr1=1, cv1=False, shr=True, shs=False, sh1=True, addpos=0, cfirst=True, warm=5, pool=())
 HALF = 512
 TILES = T // P
 PASSES = D // 512
@@ -37,7 +37,6 @@ def tile_cachetocachegatedkeyfuser_w4_kernel(
         ctx.enter_context(tc.manual_schedule())
 
         ident = keep.tile([P, P], F32, name="ident", align_bytes=64)
-        make_identity(nc, ident[:])
         warm = keep.tile([P, 1], F32, name="warm")
         nc.vector.memset(warm[:], 0.0)
         nc.scalar.activation(out=warm[:], in_=warm[:], func=ACT.Silu)
@@ -54,13 +53,17 @@ def tile_cachetocachegatedkeyfuser_w4_kernel(
         kr_in = {}
         ks_in = {}
 
-        def load_recv(i):
-            kr_in[i] = inp.tile([P, D], BF16, name="kr", align_bytes=64)
-            nc.sync.dma_start(out=kr_in[i][:], in_=k_recv[i * P : (i + 1) * P, :])
+        def load_recv(i, n=1, queue=nc.sync):
+            t = inp.tile([P, n, D], BF16, name="kr%d" % i, bufs=1, align_bytes=64)
+            queue.dma_start(out=t[:], in_=k_recv[i * P : (i + n) * P, :].rearrange("(n p) d -> p n d", p=P))
+            for j in range(n):
+                kr_in[i + j] = t[:, j, :]
 
-        def load_share(i):
-            ks_in[i] = inp.tile([P, D], U8, name="kb", align_bytes=64)
-            nc.sync.dma_start(out=ks_in[i][:], in_=k_share_bytes[i * P : (i + 1) * P, :])
+        def load_share(i, n=1):
+            t = inp.tile([P, n, D], U8, name="kb%d" % i, bufs=1, align_bytes=64)
+            nc.sync.dma_start(out=t[:], in_=k_share_bytes[i * P : (i + n) * P, :].rearrange("(n p) d -> p n d", p=P))
+            for j in range(n):
+                ks_in[i + j] = t[:, j, :]
 
         def load_words(nm, w_words):
             nc.sync.dma_start(
@@ -78,40 +81,40 @@ def tile_cachetocachegatedkeyfuser_w4_kernel(
         gcol = keep.tile([P, 8], BF16, name="gcol")
 
         def load_kscale():
-            nc.sync.dma_start(
+            nc.gpsimd.dma_start(
                 out=kscale[:].rearrange("p (g t) -> p g t", t=4),
                 in_=k_share_scale.rearrange("o (g p t) -> p (o g) t", p=P, t=4),
             )
 
         def load_gain():
-            nc.sync.dma_start(out=gcol[:], in_=g_hid.rearrange("(n m) -> n m", m=8))
+            nc.gpsimd.dma_start(out=gcol[:], in_=g_hid.rearrange("(n m) -> n m", m=8))
 
-        load_share(0)
-        load_recv(0)
         load_kscale()
+        load_gain()
+        make_identity(nc, ident[:])
+        load_share(0, CFG["ks0"])
+        load_recv(0)
         load_scales("recv", w_recv_scales)
         load_words("recv", w_recv_words)
         if CFG["ld1"] == 0:
             load_recv(1)
-            load_share(1)
+            if CFG["ks0"] == 1:
+                load_share(1)
         load_words("share", w_share_words)
         load_scales("share", w_share_scales)
         if CFG["ld1"] == 1:
             load_recv(1)
-            load_share(1)
-        load_gain()
-        for i in (2, 3):
-            load_recv(i)
-            load_share(i)
+            if CFG["ks0"] == 1:
+                load_share(1)
+        load_recv(2, 2)
+        load_share(2, 2)
         load_words("gate", w_gate_words)
         load_scales("gate", w_gate_scales)
-        load_recv(4)
-        load_share(4)
+        load_share(4, 4)
+        load_recv(4, 2)
         load_words("delta", w_delta_words)
         load_scales("delta", w_delta_scales)
-        for i in range(5, TILES):
-            load_recv(i)
-            load_share(i)
+        load_recv(6, 2)
         ksb = {}
         krs = {}
         kss = {}
@@ -127,46 +130,46 @@ def tile_cachetocachegatedkeyfuser_w4_kernel(
         prd = {}
         res = {}
 
-        def cast_share(i):
+        def cast_share(i, on_vector=False):
             t = work.tile([P, D], BF16, name="ksb", align_bytes=64)
-            nc.scalar.copy(out=t[:], in_=ks_in[i][:].bitcast(FP8))
+            (nc.vector.tensor_copy if on_vector else nc.scalar.copy)(out=t[:], in_=ks_in[i].bitcast(FP8))
             ksb[i] = t
 
         def shuffle_recv(i):
             t = work.tile([P, D], BF16, name="krs", align_bytes=64)
             nc.scalar.copy(
-                out=t[:].bitcast(F32).rearrange("p (u x) -> p u x", u=2),
-                in_=kr_in[i][:].bitcast(F32).rearrange("p (x u) -> p u x", u=2),
+                out=t[:].bitcast(F32).rearrange("p (g u m) -> p g u m", g=2, u=2),
+                in_=kr_in[i].bitcast(F32).rearrange("p (g m u) -> p g u m", g=2, u=2),
             )
             krs[i] = t
 
         def shuffle_share(i):
             t = work.tile([P, D], BF16, name="kss", align_bytes=64)
             nc.scalar.copy(
-                out=t[:].bitcast(F32).rearrange("p (u x) -> p u x", u=2),
-                in_=ksb[i][:].bitcast(F32).rearrange("p (x u) -> p u x", u=2),
+                out=t[:].bitcast(F32).rearrange("p (g u m) -> p g u m", g=2, u=2),
+                in_=ksb[i][:].bitcast(F32).rearrange("p (g m u) -> p g u m", g=2, u=2),
             )
             kss[i] = t
 
         def transpose_recv(i):
             if i in krs:
-                transpose_words(krs[i], True, ("r", i))
+                transpose_words(krs[i][:], True, ("r", i))
             else:
                 transpose_words(kr_in[i], False, ("r", i))
 
         def transpose_share(i):
             if i in kss:
-                transpose_words(kss[i], True, ("s", i))
+                transpose_words(kss[i][:], True, ("s", i))
             else:
-                transpose_words(ksb[i], False, ("s", i))
+                transpose_words(ksb[i][:], False, ("s", i))
 
         def transpose_words(src, shuffled, key):
             bank = psum.tile([P, 4, P], F32, name="tr", bufs=3)
-            w = src[:].bitcast(F32)
+            w = src.bitcast(F32)
             for g in range(PASSES):
                 for u in range(2):
                     if shuffled:
-                        blk = w[:, (2 * u + g) * P : (2 * u + g + 1) * P]
+                        blk = w[:, (2 * g + u) * P : (2 * g + u + 1) * P]
                     else:
                         blk = w[:, 256 * g + u : 256 * (g + 1) : 2]
                     nc.tensor.transpose(bank[:, 2 * u + g, :], blk, ident[:])
@@ -180,6 +183,19 @@ def tile_cachetocachegatedkeyfuser_w4_kernel(
 
         def new_xg(i):
             xg[i] = work.tile([P, 2 * D], BF16, name="xg", align_bytes=64)
+
+        def copy_quant_recv_by_pass(i):
+            c, s = xc[i]
+            for g in range(PASSES):
+                nc.vector.tensor_copy(
+                    out=xg[i][:, HALF * g : HALF * (g + 1)].bitcast(F32).rearrange("p (r u) -> p r u", u=2),
+                    in_=trp["r", i][:].rearrange("p (u g) r -> p g r u", u=2)[:, g],
+                )
+            for g in range(PASSES):
+                nc.vector.quantize_mx(
+                    out=c[:, P * g : P * (g + 1)].bitcast(FP8X4), scales=s[:, P * g : P * (g + 1)],
+                    in_=xg[i][:, HALF * g : HALF * (g + 1)],
+                )
 
         def copy_recv(i, on_vector=False):
             copy_out(nc.vector.tensor_copy if on_vector else nc.scalar.copy, trp["r", i], xg[i][:, 0:D])
@@ -206,23 +222,26 @@ def tile_cachetocachegatedkeyfuser_w4_kernel(
 
         def new_up(i):
             for h in range(2):
-                up[i, h] = psum.tile([P, HALF], F32, name="up", bufs=2)
+                up[i, h] = psum.tile([P, HALF], F32, name="acc", bufs=5)
 
-        def mm_up(i, h, srcs):
+        def mm_up_pass(i, h, si, g):
             c, s = xc[i]
-            for si in srcs:
-                nm = ("recv", "share")[si]
+            nm = ("recv", "share")[si]
+            col = slice(256 * si + P * g, 256 * si + P * (g + 1))
+            nc.tensor.matmul_mx(
+                out=up[i, h][:],
+                lhsT=c[:, col].bitcast(FP8X4),
+                lhsT_scale=s[:, col],
+                rhs=words[nm][:, g, 2 * HALF * h : 2 * HALF * (h + 1)].bitcast(FP4X4),
+                rhs_scale=scales[nm][:, g, HALF * h : HALF * (h + 1)],
+                start=(si == 0 and g == 0),
+                stop=(si == 1 and g == PASSES - 1),
+            )
+
+        def mm_up(i, h):
+            for si in range(2):
                 for g in range(PASSES):
-                    col = slice(256 * si + P * g, 256 * si + P * (g + 1))
-                    nc.tensor.matmul_mx(
-                        out=up[i, h][:],
-                        lhsT=c[:, col].bitcast(FP8X4),
-                        lhsT_scale=s[:, col],
-                        rhs=words[nm][:, g, 2 * HALF * h : 2 * HALF * (h + 1)].bitcast(FP4X4),
-                        rhs_scale=scales[nm][:, g, HALF * h : HALF * (h + 1)],
-                        start=(si == 0 and g == 0),
-                        stop=(si == 1 and g == PASSES - 1),
-                    )
+                    mm_up_pass(i, h, si, g)
 
         sl = {}
 
@@ -230,7 +249,7 @@ def tile_cachetocachegatedkeyfuser_w4_kernel(
             if h == 0:
                 sl[i] = work.tile([P, F], F32, name="sl", bufs=3, align_bytes=64)
             nc.scalar.activation(
-                out=sl[i][:].rearrange("p (u g m e) -> p g u m e", u=2, g=2, e=2)[:, h],
+                out=sl[i][:, HALF * h : HALF * (h + 1)].rearrange("p (u m e) -> p u m e", u=2, e=2),
                 in_=up[i, h][:].rearrange("p (m u e) -> p u m e", u=2, e=2),
                 func=ACT.Silu,
             )
@@ -250,10 +269,7 @@ def tile_cachetocachegatedkeyfuser_w4_kernel(
             hc[i] = (c, s)
 
         def mm_out(i, nm, h):
-            if i == TILES - 1 and nm == "gate":
-                bank = psum.tile([P, HALF], F32, name="up", bufs=2)
-            else:
-                bank = psum.tile([P, HALF], F32, name="gd", bufs=3)
+            bank = psum.tile([P, HALF], F32, name="acc", bufs=5)
             c, s = hc[i]
             for g in range(PASSES):
                 col = slice(P * g, P * (g + 1))
@@ -272,21 +288,37 @@ def tile_cachetocachegatedkeyfuser_w4_kernel(
             t = work.tile([P, HALF], F32, name="th", align_bytes=64)
             nc.scalar.activation(out=t[:], in_=gd[i, "gate", h][:], func=ACT.Tanh, scale=0.5)
             th[i, h] = t
+            if i in on_pool:
+                s = work.tile([P, HALF], F32, name="sg", align_bytes=64)
+                nc.scalar.activation(out=s[:], in_=t[:], func=ACT.Copy, scale=0.5, bias=0.5)
+                th[i, h] = s
+
+        on_pool = CFG["pool"]
 
         def gate_delta(i, h):
             if h == 0:
                 prd[i] = work.tile([P, D], F32, name="prd", bufs=3, align_bytes=64)
-            nc.vector.scalar_tensor_tensor(
-                out=prd[i][:, HALF * h : HALF * (h + 1)], in0=th[i, h][:], scalar=1.0, in1=gd[i, "delta", h][:], op0=ALU.add, op1=ALU.mult
-            )
+            if i in on_pool:
+                nc.vector.tensor_tensor(
+                    out=prd[i][:, HALF * h : HALF * (h + 1)], in0=th[i, h][:], in1=gd[i, "delta", h][:], op=ALU.mult
+                )
+            else:
+                nc.vector.scalar_tensor_tensor(
+                    out=prd[i][:, HALF * h : HALF * (h + 1)], in0=th[i, h][:], scalar=1.0, in1=gd[i, "delta", h][:], op0=ALU.add, op1=ALU.mult
+                )
 
         def add_store(i, c0=0, c1=D):
             if c0 == 0:
                 res[i] = work.tile([P, D], F32, name="res", bufs=3, align_bytes=64)
-            nc.vector.scalar_tensor_tensor(
-                out=res[i][:, c0:c1], in0=prd[i][:, c0:c1], scalar=0.5, in1=kr_in[i][:, c0:c1],
-                op0=ALU.mult, op1=ALU.add,
-            )
+            if i in on_pool:
+                nc.gpsimd.tensor_tensor(
+                    out=res[i][:, c0:c1], in0=prd[i][:, c0:c1], in1=kr_in[i][:, c0:c1], op=ALU.add
+                )
+            else:
+                nc.vector.scalar_tensor_tensor(
+                    out=res[i][:, c0:c1], in0=prd[i][:, c0:c1], scalar=0.5, in1=kr_in[i][:, c0:c1],
+                    op0=ALU.mult, op1=ALU.add,
+                )
             nc.sync.dma_start(out=out[i * P : (i + 1) * P, c0:c1], in_=res[i][:, c0:c1])
 
         gfull = keep.tile([P, F], BF16, name="gfull", align_bytes=64)
@@ -298,130 +330,120 @@ def tile_cachetocachegatedkeyfuser_w4_kernel(
                 nc.tensor.transpose(gbank[:, m, :], gw[:, m : m + 1].to_broadcast([P, P]), ident[:])
             for g in range(PASSES):
                 nc.vector.tensor_copy(
-                    out=gfull[:].bitcast(F32).rearrange("p (u g n a) -> p g u n a", u=2, g=2, a=2)[:, g],
+                    out=gfull[:, HALF * g : HALF * (g + 1)].bitcast(F32).rearrange("p (u n a) -> p u n a", u=2, a=2),
                     in_=gbank[:, :, 64 * g : 64 * (g + 1)].rearrange("p (a u) n -> p u n a", u=2),
                 )
 
-        cast_share(0)
+        if CFG["warm"]:
+            zero = keep.tile([P, HALF], BF16, name="zero", align_bytes=64)
+            nc.vector.memset(zero[:], 0.0)
+            wb = psum.tile([P, HALF], F32, name="acc", bufs=5)
+            for n in range(CFG["warm"]):
+                nc.tensor.matmul(wb[:], lhsT=zero[:, 0:P], rhs=zero[:], start=True, stop=True)
+        cv = CFG["castv"]
+        cast_share(0, cv >= 1)
+        if cv >= 2:
+            cast_share(1, True)
         transpose_recv(0)
         transpose_share(0)
-        new_xg(0)
-        new_xc(0)
-        new_xg(1)
-        new_xc(1)
-        copy_recv(0, on_vector=True)
-        quant_x(0, 0, 1)
+        for i in range(2):
+            new_xg(i)
+            new_xc(i)
+        copy_quant_recv_by_pass(0)
         scale_share(0)
-        quant_x(0, 1, 2)
-        new_up(0)
         if CFG["shr"] and CFG["sh1"]:
             shuffle_recv(1)
-        cast_share(1)
-        if CFG["shs"] and CFG["sh1"]:
-            shuffle_share(1)
-        if CFG["tr1"] == 0:
-            transpose_recv(1)
-            transpose_share(1)
-        mm_up(0, 0, (0,))
-        mm_up(0, 1, (0,))
-        if CFG["tr1"] == 1:
-            transpose_recv(1)
-            transpose_share(1)
-        copy_recv(1, on_vector=CFG["cv1"])
-        scale_share(1)
-        quant_x(1, 0, 2)
-        mm_up(0, 0, (1,))
-        mm_up(0, 1, (1,))
-        if CFG["shr"]:
+        if cv < 2:
+            cast_share(1, False)
+        if CFG["shr"] and CFG["sh2e"]:
             shuffle_recv(2)
-        cast_share(2)
-        if CFG["shs"]:
-            shuffle_share(2)
+        new_up(0)
+        for g in range(PASSES):
+            for h in range(2):
+                mm_up_pass(0, h, 0, g)
+        transpose_recv(1)
+        transpose_share(1)
+        copy_recv(1, on_vector=CFG["cv1"])
+        quant_x(0, 1, 2)
+        scale_share(1)
+        for g in range(PASSES):
+            for h in range(2):
+                mm_up_pass(0, h, 1, g)
+        if CFG["shr"] and not CFG["sh2e"]:
+            shuffle_recv(2)
+        cast_share(2, cv >= 3)
+        quant_x(1, 0, 2)
         spread_gain()
         silu(0, 0)
         silu(0, 1)
         gain(0)
         for i in range(1, TILES + 1):
-            hs_now = [i - 2] if 2 <= i < TILES else []
-            if i == TILES - 1:
-                hs_now = [i - 2, i - 1]
-            if i == TILES:
-                hs_now = [TILES - 1]
+            h_now = [] if i == 1 else [i - 2] if i < CFG["cu"] else [i - 2, i - 1] if i == CFG["cu"] else [i - 1]
+            if i == 1:
+                out_now = []
+            elif i < CFG["cu"]:
+                out_now = [(i - 2, 0), (i - 2, 1)]
+            elif i == CFG["cu"]:
+                out_now = [(i - 2, 0), (i - 2, 1), (i - 1, 0)]
+            elif i == TILES:
+                out_now = [(i - 2, 1), (i - 1, 0), (i - 1, 1)]
+            else:
+                out_now = [(i - 2, 1), (i - 1, 0)]
             xn = i + 1 if i + 1 < TILES else None
             xs = i + 2 if i + 2 < TILES else None
-            for j in hs_now:
-                transpose_words(hs[j], True, ("h", j))
+            for j in h_now[:-1]:
+                transpose_words(hs[j][:], True, ("h", j))
             if xn is not None:
                 transpose_recv(xn)
                 transpose_share(xn)
                 new_xg(xn)
                 new_xc(xn)
-            if i == 1 and CFG["late1"]:
-                pass
-            for j in hs_now:
+            for j in h_now[:-1]:
                 copy_h(j)
+                quant_h(j)
             if xn is not None:
                 copy_recv(xn)
-            for j in hs_now:
-                quant_h(j)
-            if xs is not None and CFG["castpos"] == 0:
-                cast_share(xs)
-            if CFG["shr"] and xs is not None and CFG["shpos"] == 2:
-                shuffle_recv(xs)
-            if CFG["shs"] and xs is not None and CFG["shpos"] == 2:
-                shuffle_share(xs)
+            for j in h_now[-1:]:
+                transpose_words(hs[j][:], True, ("h", j))
+                copy_h(j)
+            if xs is not None:
+                if CFG["cfirst"]:
+                    cast_share(xs)
+                if CFG["shr"]:
+                    shuffle_recv(xs)
+                if not CFG["cfirst"]:
+                    cast_share(xs)
+                if CFG["shs"]:
+                    shuffle_share(xs)
             if xn is not None:
                 scale_share(xn)
+            if CFG["addpos"] == 0 and 3 <= i < TILES:
+                add_store(i - 3)
+            for j in h_now[-1:]:
+                quant_h(j)
+            if i == TILES:
+                add_store(i - 3, HALF, D)
+            if CFG["addpos"] == 1 and 3 <= i < TILES:
+                add_store(i - 3)
+            if xn is not None:
                 quant_x(xn, 0, 2)
             if i < TILES:
                 new_up(i)
-                mm_up(i, 0, (0, 1))
+                mm_up(i, 0)
                 silu(i, 0)
-                if i >= 3 and CFG["addpos"] == 0:
-                    add_store(i - 3)
-                mm_up(i, 1, (0, 1))
-                if xs is not None and CFG["castpos"] == 1:
-                    cast_share(xs)
-                if CFG["shr"] and xs is not None and CFG["shpos"] == 3:
-                    shuffle_recv(xs)
-                if CFG["shs"] and xs is not None and CFG["shpos"] == 3:
-                    shuffle_share(xs)
+                mm_up(i, 1)
                 silu(i, 1)
-                if i >= 3 and CFG["addpos"] == 1:
-                    add_store(i - 3)
+                if i == TILES - 1:
+                    add_store(i - 2, 0, HALF)
                 gain(i)
-            last = [i - 2] if 2 <= i < TILES else ([TILES - 2, TILES - 1] if i == TILES else [])
-            if CFG["shr"] and xs is not None and CFG["shpos"] == 0:
-                shuffle_recv(xs)
-            if CFG["shs"] and xs is not None and CFG["shpos"] == 0:
-                shuffle_share(xs)
-            for j in last:
-                if i == TILES and j == TILES - 2:
+            for n, (j, h) in enumerate(out_now):
+                mm_out(j, "gate", h)
+                tanh(j, h)
+                mm_out(j, "delta", h)
+                gate_delta(j, h)
+                if i == TILES and n == 1:
                     add_store(j - 1)
-                if CFG["gd"] == 0 or j == TILES - 1:
-                    mm_out(j, "gate", 0)
-                    tanh(j, 0)
-                    mm_out(j, "delta", 0)
-                    if j == TILES - 1:
-                        add_store(j - 1)
-                    gate_delta(j, 0)
-                    if j == TILES - 1:
-                        add_store(j, 0, HALF)
-                    mm_out(j, "gate", 1)
-                    tanh(j, 1)
-                    mm_out(j, "delta", 1)
-                    gate_delta(j, 1)
-                else:
-                    mm_out(j, "gate", 0)
-                    tanh(j, 0)
-                    mm_out(j, "gate", 1)
-                    tanh(j, 1)
-                    mm_out(j, "delta", 0)
-                    gate_delta(j, 0)
-                    mm_out(j, "delta", 1)
-                    gate_delta(j, 1)
-            if CFG["shr"] and xs is not None and CFG["shpos"] == 1:
-                shuffle_recv(xs)
-            if CFG["shs"] and xs is not None and CFG["shpos"] == 1:
-                shuffle_share(xs)
+                if i == TILES - 1 and n == 1:
+                    pass
+        add_store(TILES - 1, 0, HALF)
         add_store(TILES - 1, HALF, D)

@@ -18,432 +18,403 @@ ACT = mybir.ActivationFunctionType
 ALU = mybir.AluOpType
 
 P = 128
-CFG = dict(cu=3, ks0=2, castv=3, sh2e=False, ld1=0, tr1=1, cv1=False, shr=True, shs=False, sh1=True, addpos=0, cfirst=True, warm=5, pool=())
-HALF = 512
 TILES = T // P
-PASSES = D // 512
+LAST = TILES - 1
+K_PASS = 512
+PASSES = D // K_PASS
+HALF = 512
+RECV, SHARE = 0, 1
+GATE, DELTA = "gate", "delta"
+WARM_UP = 4
+ORDERED_FROM = 3
 
 
 def tile_cachetocachegatedkeyfuser_w4_kernel(
-    tc, k_recv, k_share_bytes, k_share_scale, w_recv_words, w_recv_scales, w_share_words, w_share_scales,
-    g_hid, w_delta_words, w_delta_scales, w_gate_words, w_gate_scales, out,
+    tc,
+    k_recv,
+    k_share_bytes,
+    k_share_scale,
+    w_recv_words,
+    w_recv_scales,
+    w_share_words,
+    w_share_scales,
+    g_hid,
+    w_delta_words,
+    w_delta_scales,
+    w_gate_words,
+    w_gate_scales,
+    out,
 ):
     nc = tc.nc
+
     with ExitStack() as ctx:
         keep = ctx.enter_context(tc.tile_pool(name="keep", bufs=1))
-        inp = ctx.enter_context(tc.tile_pool(name="inp", bufs=TILES))
         work = ctx.enter_context(tc.tile_pool(name="work", bufs=3))
-        psum = ctx.enter_context(tc.psum_pool(name="psum", bufs=2))
+        psum = ctx.enter_context(tc.psum_pool(name="psum", bufs=1))
         ctx.enter_context(tc.manual_schedule())
 
+        zeros = keep.tile([P, HALF], BF16, name="zeros", align_bytes=64)
+        nc.gpsimd.memset(zeros[:], 0.0)
         ident = keep.tile([P, P], F32, name="ident", align_bytes=64)
-        warm = keep.tile([P, 1], F32, name="warm")
-        nc.vector.memset(warm[:], 0.0)
-        nc.scalar.activation(out=warm[:], in_=warm[:], func=ACT.Silu)
+        make_identity(nc, ident[:])
+
+        first = keep.tile([P, 1], F32, name="first")
+        nc.vector.memset(first[:], 0.0)
+        nc.scalar.activation(out=first[:], in_=first[:], func=ACT.Silu)
 
         words = {}
         scales = {}
-        for nm in ("recv", "share", "gate", "delta"):
-            wt = keep.tile([P, PASSES, 2 * F], U8, name="words_" + nm, align_bytes=256)
-            st = keep.tile([P, PASSES, F], U8, name="scales_" + nm, align_bytes=256)
-            nc.vector.memset(st[:].rearrange("p g n -> p (g n)").bitcast(I32), 0)
-            words[nm] = wt
-            scales[nm] = st
+        for name in (RECV, SHARE, GATE, DELTA):
+            words[name] = keep.tile([P, PASSES, 2 * F], U8, name="words_%s" % name, align_bytes=256)
+            scales[name] = keep.tile([P, PASSES, F], U8, name="scales_%s" % name, align_bytes=256)
+            nc.vector.memset(scales[name][:].rearrange("p g n -> p (g n)").bitcast(I32), 0)
 
-        kr_in = {}
-        ks_in = {}
+        def load_words(name, w_words):
+            nc.sync.dma_start(out=words[name][:].bitcast(I32), in_=w_words.bitcast(I32).rearrange("g p n -> p g n"))
 
-        def load_recv(i, n=1, queue=nc.sync):
-            t = inp.tile([P, n, D], BF16, name="kr%d" % i, bufs=1, align_bytes=64)
-            queue.dma_start(out=t[:], in_=k_recv[i * P : (i + n) * P, :].rearrange("(n p) d -> p n d", p=P))
-            for j in range(n):
-                kr_in[i + j] = t[:, j, :]
-
-        def load_share(i, n=1):
-            t = inp.tile([P, n, D], U8, name="kb%d" % i, bufs=1, align_bytes=64)
-            nc.sync.dma_start(out=t[:], in_=k_share_bytes[i * P : (i + n) * P, :].rearrange("(n p) d -> p n d", p=P))
-            for j in range(n):
-                ks_in[i + j] = t[:, j, :]
-
-        def load_words(nm, w_words):
-            nc.sync.dma_start(
-                out=words[nm][:].bitcast(I32), in_=w_words.bitcast(I32).rearrange("g p n -> p g n")
-            )
-
-        def load_scales(nm, w_scales):
-            sc = w_scales.bitcast(I32).rearrange("g q n -> q g n")
+        def load_scales(name, w_scales):
+            rows = w_scales.bitcast(I32).rearrange("g q n -> q g n")
             for q in range(4):
                 nc.sync.dma_start(
-                    out=scales[nm][32 * q : 32 * q + 4, :, :].bitcast(I32), in_=sc[4 * q : 4 * q + 4, :, :]
+                    out=scales[name][32 * q : 32 * q + 4, :, :].bitcast(I32), in_=rows[4 * q : 4 * q + 4, :, :]
                 )
 
-        kscale = keep.tile([P, 4 * PASSES], F32, name="kscale")
-        gcol = keep.tile([P, 8], BF16, name="gcol")
+        recv = {}
+        share_bytes = {}
 
-        def load_kscale():
-            nc.gpsimd.dma_start(
-                out=kscale[:].rearrange("p (g t) -> p g t", t=4),
+        def load_recv(i, count):
+            t = keep.tile([P, count, D], BF16, name="recv_%d" % i, align_bytes=64)
+            nc.sync.dma_start(out=t[:], in_=k_recv[i * P : (i + count) * P, :].rearrange("(n p) d -> p n d", p=P))
+            for n in range(count):
+                recv[i + n] = t[:, n, :]
+
+        def load_share(i, count):
+            t = keep.tile([P, count, D], U8, name="share_bytes_%d" % i, align_bytes=64)
+            nc.sync.dma_start(
+                out=t[:], in_=k_share_bytes[i * P : (i + count) * P, :].rearrange("(n p) d -> p n d", p=P)
+            )
+            for n in range(count):
+                share_bytes[i + n] = t[:, n, :]
+
+        share_scale = keep.tile([P, 4 * PASSES], F32, name="share_scale")
+
+        def load_share_scale():
+            nc.sync.dma_start(
+                out=share_scale[:].rearrange("p (g t) -> p g t", t=4),
                 in_=k_share_scale.rearrange("o (g p t) -> p (o g) t", p=P, t=4),
             )
 
-        def load_gain():
-            nc.gpsimd.dma_start(out=gcol[:], in_=g_hid.rearrange("(n m) -> n m", m=8))
+        gain_rows = keep.tile([P, 8], BF16, name="gain_rows")
 
-        load_kscale()
+        def load_gain():
+            nc.sync.dma_start(out=gain_rows[:], in_=g_hid.rearrange("(n m) -> n m", m=8))
+
+        load_recv(0, 1)
+        load_share(0, 2)
+        load_share_scale()
+        load_scales(RECV, w_recv_scales)
+        load_words(RECV, w_recv_words)
+        load_recv(1, 1)
+        load_words(SHARE, w_share_words)
+        load_scales(SHARE, w_share_scales)
         load_gain()
-        make_identity(nc, ident[:])
-        load_share(0, CFG["ks0"])
-        load_recv(0)
-        load_scales("recv", w_recv_scales)
-        load_words("recv", w_recv_words)
-        if CFG["ld1"] == 0:
-            load_recv(1)
-            if CFG["ks0"] == 1:
-                load_share(1)
-        load_words("share", w_share_words)
-        load_scales("share", w_share_scales)
-        if CFG["ld1"] == 1:
-            load_recv(1)
-            if CFG["ks0"] == 1:
-                load_share(1)
-        load_recv(2, 2)
         load_share(2, 2)
-        load_words("gate", w_gate_words)
-        load_scales("gate", w_gate_scales)
+        load_recv(2, 1)
+        load_recv(3, 1)
+        load_words(GATE, w_gate_words)
+        load_scales(GATE, w_gate_scales)
         load_share(4, 4)
         load_recv(4, 2)
-        load_words("delta", w_delta_words)
-        load_scales("delta", w_delta_scales)
+        load_words(DELTA, w_delta_words)
+        load_scales(DELTA, w_delta_scales)
         load_recv(6, 2)
-        ksb = {}
-        krs = {}
-        kss = {}
-        trp = {}
-        xg = {}
-        xc = {}
-        up = {}
-        hs = {}
-        hg = {}
-        hc = {}
-        gd = {}
-        th = {}
-        prd = {}
-        res = {}
 
-        def cast_share(i, on_vector=False):
-            t = work.tile([P, D], BF16, name="ksb", align_bytes=64)
-            (nc.vector.tensor_copy if on_vector else nc.scalar.copy)(out=t[:], in_=ks_in[i].bitcast(FP8))
-            ksb[i] = t
+        ordered_recv = {}
+        ordered_share = {}
+        share = {}
+        turned = {}
 
-        def shuffle_recv(i):
-            t = work.tile([P, D], BF16, name="krs", align_bytes=64)
+        def widen_share(i, engine_copy):
+            share[i] = work.tile([P, D], BF16, name="share", align_bytes=64)
+            engine_copy(out=share[i][:], in_=share_bytes[i].bitcast(FP8))
+
+        def order_words(src, name):
+            t = work.tile([P, D], BF16, name=name, align_bytes=64)
             nc.scalar.copy(
-                out=t[:].bitcast(F32).rearrange("p (g u m) -> p g u m", g=2, u=2),
-                in_=kr_in[i].bitcast(F32).rearrange("p (g m u) -> p g u m", g=2, u=2),
+                out=t[:].bitcast(F32).rearrange("p (g u m) -> p g u m", g=PASSES, u=2),
+                in_=src.bitcast(F32).rearrange("p (g m u) -> p g u m", g=PASSES, u=2),
             )
-            krs[i] = t
+            return t
 
-        def shuffle_share(i):
-            t = work.tile([P, D], BF16, name="kss", align_bytes=64)
-            nc.scalar.copy(
-                out=t[:].bitcast(F32).rearrange("p (g u m) -> p g u m", g=2, u=2),
-                in_=ksb[i][:].bitcast(F32).rearrange("p (g m u) -> p g u m", g=2, u=2),
-            )
-            kss[i] = t
-
-        def transpose_recv(i):
-            if i in krs:
-                transpose_words(krs[i][:], True, ("r", i))
-            else:
-                transpose_words(kr_in[i], False, ("r", i))
-
-        def transpose_share(i):
-            if i in kss:
-                transpose_words(kss[i][:], True, ("s", i))
-            else:
-                transpose_words(ksb[i][:], False, ("s", i))
-
-        def transpose_words(src, shuffled, key):
-            bank = psum.tile([P, 4, P], F32, name="tr", bufs=3)
+        def turn(src, ordered, key):
+            bank = psum.tile([P, 4, P], F32, name="turned", bufs=3)
             w = src.bitcast(F32)
             for g in range(PASSES):
                 for u in range(2):
-                    if shuffled:
-                        blk = w[:, (2 * g + u) * P : (2 * g + u + 1) * P]
+                    if ordered:
+                        block = w[:, (2 * g + u) * P : (2 * g + u + 1) * P]
                     else:
-                        blk = w[:, 256 * g + u : 256 * (g + 1) : 2]
-                    nc.tensor.transpose(bank[:, 2 * u + g, :], blk, ident[:])
-            trp[key] = bank
+                        block = w[:, 2 * P * g + u : 2 * P * (g + 1) : 2]
+                    nc.tensor.transpose(bank[:, 2 * u + g, :], block, ident[:])
+            turned[key] = bank
 
-        def copy_out(eng_copy, bank, dst):
-            eng_copy(
+        def turn_recv(i):
+            if i >= ORDERED_FROM:
+                turn(ordered_recv[i][:], True, (RECV, i))
+            else:
+                turn(recv[i], False, (RECV, i))
+
+        def turn_share(i):
+            if i >= ORDERED_FROM:
+                turn(ordered_share[i][:], True, (SHARE, i))
+            else:
+                turn(share[i][:], False, (SHARE, i))
+
+        def interleave(engine_copy, key, dst):
+            engine_copy(
                 out=dst.bitcast(F32).rearrange("p (x u) -> p x u", u=2),
-                in_=bank[:].rearrange("p (u g) r -> p (g r) u", u=2),
+                in_=turned[key][:].rearrange("p (u g) r -> p (g r) u", u=2),
             )
 
-        def new_xg(i):
-            xg[i] = work.tile([P, 2 * D], BF16, name="xg", align_bytes=64)
+        x = {}
+        x_codes = {}
+        x_scales = {}
 
-        def copy_quant_recv_by_pass(i):
-            c, s = xc[i]
-            for g in range(PASSES):
-                nc.vector.tensor_copy(
-                    out=xg[i][:, HALF * g : HALF * (g + 1)].bitcast(F32).rearrange("p (r u) -> p r u", u=2),
-                    in_=trp["r", i][:].rearrange("p (u g) r -> p g r u", u=2)[:, g],
-                )
-            for g in range(PASSES):
-                nc.vector.quantize_mx(
-                    out=c[:, P * g : P * (g + 1)].bitcast(FP8X4), scales=s[:, P * g : P * (g + 1)],
-                    in_=xg[i][:, HALF * g : HALF * (g + 1)],
-                )
+        def new_x(i):
+            x[i] = work.tile([P, 2 * D], BF16, name="x", align_bytes=64)
+            x_codes[i] = work.tile([P, 2 * D // 4], U32, name="x_codes", align_bytes=64)
+            x_scales[i] = work.tile([P, 2 * D // 4], U8, name="x_scales", align_bytes=64)
 
-        def copy_recv(i, on_vector=False):
-            copy_out(nc.vector.tensor_copy if on_vector else nc.scalar.copy, trp["r", i], xg[i][:, 0:D])
+        def quantise_x(i, start, stop):
+            c = slice(start // 4, stop // 4)
+            nc.vector.quantize_mx(
+                out=x_codes[i][:, c].bitcast(FP8X4), scales=x_scales[i][:, c], in_=x[i][:, start:stop]
+            )
 
         def scale_share(i):
-            v = trp["s", i][:].rearrange("p a r -> p (a r)").bitcast(BF16)
-            v = v.rearrange("p (u g r e) -> p g r u e", g=2, u=2, e=2)
-            o = xg[i][:, D : 2 * D].rearrange("p (g r u e) -> p g r u e", g=2, u=2, e=2)
-            s = kscale[:].rearrange("p (g u e) -> p g u e", u=2, e=2)
+            v = turned[SHARE, i][:].rearrange("p a r -> p (a r)").bitcast(BF16)
+            s = share_scale[:].rearrange("p (g u e) -> p g u e", u=2, e=2)
             nc.vector.tensor_tensor(
-                out=o, in0=v, in1=s.unsqueeze(2).to_broadcast([P, PASSES, P, 2, 2]), op=ALU.mult
+                out=x[i][:, D : 2 * D].rearrange("p (g r u e) -> p g r u e", g=PASSES, u=2, e=2),
+                in0=v.rearrange("p (u g r e) -> p g r u e", u=2, g=PASSES, e=2),
+                in1=s.unsqueeze(2).to_broadcast([P, PASSES, P, 2, 2]),
+                op=ALU.mult,
             )
 
-        def new_xc(i):
-            c = work.tile([P, 512], U32, name="xc", align_bytes=64)
-            s = work.tile([P, 512], U8, name="xs", align_bytes=64)
-            xc[i] = (c, s)
+        u_bank = {}
 
-        def quant_x(i, a, b):
-            c, s = xc[i]
-            nc.vector.quantize_mx(
-                out=c[:, 256 * a : 256 * b].bitcast(FP8X4), scales=s[:, 256 * a : 256 * b], in_=xg[i][:, D * a : D * b]
-            )
-
-        def new_up(i):
+        def new_u(i):
             for h in range(2):
-                up[i, h] = psum.tile([P, HALF], F32, name="acc", bufs=5)
+                u_bank[i, h] = psum.tile([P, HALF], F32, name="sums", bufs=5)
 
-        def mm_up_pass(i, h, si, g):
-            c, s = xc[i]
-            nm = ("recv", "share")[si]
-            col = slice(256 * si + P * g, 256 * si + P * (g + 1))
+        def multiply_u(i, h, operand, g):
+            c = slice((operand * PASSES + g) * P, (operand * PASSES + g + 1) * P)
             nc.tensor.matmul_mx(
-                out=up[i, h][:],
-                lhsT=c[:, col].bitcast(FP8X4),
-                lhsT_scale=s[:, col],
-                rhs=words[nm][:, g, 2 * HALF * h : 2 * HALF * (h + 1)].bitcast(FP4X4),
-                rhs_scale=scales[nm][:, g, HALF * h : HALF * (h + 1)],
-                start=(si == 0 and g == 0),
-                stop=(si == 1 and g == PASSES - 1),
+                out=u_bank[i, h][:],
+                lhsT=x_codes[i][:, c].bitcast(FP8X4),
+                lhsT_scale=x_scales[i][:, c],
+                rhs=words[operand][:, g, 2 * HALF * h : 2 * HALF * (h + 1)].bitcast(FP4X4),
+                rhs_scale=scales[operand][:, g, HALF * h : HALF * (h + 1)],
+                start=(operand == RECV and g == 0),
+                stop=(operand == SHARE and g == PASSES - 1),
             )
 
-        def mm_up(i, h):
-            for si in range(2):
-                for g in range(PASSES):
-                    mm_up_pass(i, h, si, g)
-
-        sl = {}
+        silu_u = {}
+        hidden = {}
+        half_gain = keep.tile([P, F], BF16, name="half_gain", align_bytes=64)
 
         def silu(i, h):
             if h == 0:
-                sl[i] = work.tile([P, F], F32, name="sl", bufs=3, align_bytes=64)
+                silu_u[i] = work.tile([P, F], F32, name="silu_u", align_bytes=64)
             nc.scalar.activation(
-                out=sl[i][:, HALF * h : HALF * (h + 1)].rearrange("p (u m e) -> p u m e", u=2, e=2),
-                in_=up[i, h][:].rearrange("p (m u e) -> p u m e", u=2, e=2),
+                out=silu_u[i][:, HALF * h : HALF * (h + 1)].rearrange("p (u m e) -> p u m e", u=2, e=2),
+                in_=u_bank[i, h][:].rearrange("p (m u e) -> p u m e", u=2, e=2),
                 func=ACT.Silu,
             )
 
-        def gain(i):
-            hs[i] = work.tile([P, F], BF16, name="hs", bufs=4, align_bytes=64)
-            nc.vector.tensor_tensor(out=hs[i][:], in0=sl[i][:], in1=gfull[:], op=ALU.mult)
+        def apply_gain(i):
+            hidden[i] = work.tile([P, F], BF16, name="hidden", bufs=4, align_bytes=64)
+            nc.vector.tensor_tensor(out=hidden[i][:], in0=silu_u[i][:], in1=half_gain[:], op=ALU.mult)
 
-        def copy_h(i):
-            hg[i] = work.tile([P, F], BF16, name="hg", align_bytes=64)
-            copy_out(nc.scalar.copy, trp["h", i], hg[i][:])
+        def turn_gain():
+            rows = half_gain_rows[:].bitcast(F32)
+            bank = psum.tile([P, 4, P], F32, name="turned", bufs=3)
+            for w in range(4):
+                nc.tensor.transpose(bank[:, w, :], rows[:, w : w + 1].to_broadcast([P, P]), ident[:])
+            turned["gain"] = bank
 
-        def quant_h(i):
-            c = work.tile([P, 256], U32, name="hc", align_bytes=64)
-            s = work.tile([P, 256], U8, name="hsc", align_bytes=64)
-            nc.vector.quantize_mx(out=c[:].bitcast(FP8X4), scales=s[:], in_=hg[i][:])
-            hc[i] = (c, s)
-
-        def mm_out(i, nm, h):
-            bank = psum.tile([P, HALF], F32, name="acc", bufs=5)
-            c, s = hc[i]
+        def copy_gain():
+            rows_of_pass = P // PASSES
             for g in range(PASSES):
-                col = slice(P * g, P * (g + 1))
+                nc.vector.tensor_copy(
+                    out=half_gain[:, HALF * g : HALF * (g + 1)]
+                    .bitcast(F32)
+                    .rearrange("p (u n a) -> p u n a", u=2, a=2),
+                    in_=turned["gain"][:, :, rows_of_pass * g : rows_of_pass * (g + 1)].rearrange(
+                        "p (a u) n -> p u n a", u=2
+                    ),
+                )
+
+        y = {}
+        y_codes = {}
+        y_scales = {}
+
+        def interleave_hidden(j):
+            y[j] = work.tile([P, F], BF16, name="y", align_bytes=64)
+            interleave(nc.scalar.copy, ("hidden", j), y[j][:])
+
+        def quantise_hidden(j):
+            y_codes[j] = work.tile([P, F // 4], U32, name="y_codes", align_bytes=64)
+            y_scales[j] = work.tile([P, F // 4], U8, name="y_scales", align_bytes=64)
+            nc.vector.quantize_mx(out=y_codes[j][:].bitcast(FP8X4), scales=y_scales[j][:], in_=y[j][:])
+
+        o_bank = {}
+        tanh_v = {}
+        update = {}
+
+        def multiply_out(j, name, h):
+            bank = psum.tile([P, HALF], F32, name="sums", bufs=5)
+            for g in range(PASSES):
+                c = slice(P * g, P * (g + 1))
                 nc.tensor.matmul_mx(
                     out=bank[:],
-                    lhsT=c[:, col].bitcast(FP8X4),
-                    lhsT_scale=s[:, col],
-                    rhs=words[nm][:, g, 2 * HALF * h : 2 * HALF * (h + 1)].bitcast(FP4X4),
-                    rhs_scale=scales[nm][:, g, HALF * h : HALF * (h + 1)],
+                    lhsT=y_codes[j][:, c].bitcast(FP8X4),
+                    lhsT_scale=y_scales[j][:, c],
+                    rhs=words[name][:, g, 2 * HALF * h : 2 * HALF * (h + 1)].bitcast(FP4X4),
+                    rhs_scale=scales[name][:, g, HALF * h : HALF * (h + 1)],
                     start=(g == 0),
                     stop=(g == PASSES - 1),
                 )
-            gd[i, nm, h] = bank
+            o_bank[j, name, h] = bank
 
-        def tanh(i, h):
-            t = work.tile([P, HALF], F32, name="th", align_bytes=64)
-            nc.scalar.activation(out=t[:], in_=gd[i, "gate", h][:], func=ACT.Tanh, scale=0.5)
-            th[i, h] = t
-            if i in on_pool:
-                s = work.tile([P, HALF], F32, name="sg", align_bytes=64)
-                nc.scalar.activation(out=s[:], in_=t[:], func=ACT.Copy, scale=0.5, bias=0.5)
-                th[i, h] = s
+        def tanh(j, h):
+            tanh_v[j, h] = work.tile([P, HALF], F32, name="tanh_v", align_bytes=64)
+            nc.scalar.activation(out=tanh_v[j, h][:], in_=o_bank[j, GATE, h][:], func=ACT.Tanh)
 
-        on_pool = CFG["pool"]
-
-        def gate_delta(i, h):
-            if h == 0:
-                prd[i] = work.tile([P, D], F32, name="prd", bufs=3, align_bytes=64)
-            if i in on_pool:
-                nc.vector.tensor_tensor(
-                    out=prd[i][:, HALF * h : HALF * (h + 1)], in0=th[i, h][:], in1=gd[i, "delta", h][:], op=ALU.mult
-                )
-            else:
+        def gate_delta(j, h, parts):
+            update[j, h] = work.tile([P, HALF], F32, name="update", bufs=6, align_bytes=64)
+            for n in range(parts):
+                c = slice(HALF // parts * n, HALF // parts * (n + 1))
                 nc.vector.scalar_tensor_tensor(
-                    out=prd[i][:, HALF * h : HALF * (h + 1)], in0=th[i, h][:], scalar=1.0, in1=gd[i, "delta", h][:], op0=ALU.add, op1=ALU.mult
+                    out=update[j, h][:, c],
+                    in0=tanh_v[j, h][:, c],
+                    scalar=1.0,
+                    in1=o_bank[j, DELTA, h][:, c],
+                    op0=ALU.add,
+                    op1=ALU.mult,
                 )
 
-        def add_store(i, c0=0, c1=D):
-            if c0 == 0:
-                res[i] = work.tile([P, D], F32, name="res", bufs=3, align_bytes=64)
-            if i in on_pool:
-                nc.gpsimd.tensor_tensor(
-                    out=res[i][:, c0:c1], in0=prd[i][:, c0:c1], in1=kr_in[i][:, c0:c1], op=ALU.add
-                )
-            else:
-                nc.vector.scalar_tensor_tensor(
-                    out=res[i][:, c0:c1], in0=prd[i][:, c0:c1], scalar=0.5, in1=kr_in[i][:, c0:c1],
-                    op0=ALU.mult, op1=ALU.add,
-                )
-            nc.sync.dma_start(out=out[i * P : (i + 1) * P, c0:c1], in_=res[i][:, c0:c1])
+        def add_and_store(j, h, engine, parts):
+            result = work.tile([P, HALF], F32, name="result", bufs=6, align_bytes=64)
+            for n in range(parts):
+                c = slice(HALF // parts * n, HALF // parts * (n + 1))
+                d = slice(HALF * h + HALF // parts * n, HALF * h + HALF // parts * (n + 1))
+                engine.tensor_tensor(out=result[:, c], in0=update[j, h][:, c], in1=recv[j][:, d], op=ALU.add)
+                nc.sync.dma_start(out=out[j * P : (j + 1) * P, d], in_=result[:, c])
 
-        gfull = keep.tile([P, F], BF16, name="gfull", align_bytes=64)
+        half_gain_rows = keep.tile([P, 8], BF16, name="half_gain_rows")
+        nc.gpsimd.tensor_scalar(out=half_gain_rows[:], in0=gain_rows[:], scalar1=0.5, scalar2=None, op0=ALU.mult)
 
-        def spread_gain():
-            gw = gcol[:].bitcast(F32)
-            gbank = psum.tile([P, 4, P], F32, name="tr", bufs=3)
-            for m in range(4):
-                nc.tensor.transpose(gbank[:, m, :], gw[:, m : m + 1].to_broadcast([P, P]), ident[:])
-            for g in range(PASSES):
-                nc.vector.tensor_copy(
-                    out=gfull[:, HALF * g : HALF * (g + 1)].bitcast(F32).rearrange("p (u n a) -> p u n a", u=2, a=2),
-                    in_=gbank[:, :, 64 * g : 64 * (g + 1)].rearrange("p (a u) n -> p u n a", u=2),
-                )
+        warm_bank = psum.tile([P, HALF], F32, name="sums", bufs=5)
+        for n in range(WARM_UP):
+            nc.tensor.matmul(warm_bank[:], lhsT=zeros[:, 0:P], rhs=zeros[:], start=True, stop=True)
 
-        if CFG["warm"]:
-            zero = keep.tile([P, HALF], BF16, name="zero", align_bytes=64)
-            nc.vector.memset(zero[:], 0.0)
-            wb = psum.tile([P, HALF], F32, name="acc", bufs=5)
-            for n in range(CFG["warm"]):
-                nc.tensor.matmul(wb[:], lhsT=zero[:, 0:P], rhs=zero[:], start=True, stop=True)
-        cv = CFG["castv"]
-        cast_share(0, cv >= 1)
-        if cv >= 2:
-            cast_share(1, True)
-        transpose_recv(0)
-        transpose_share(0)
-        for i in range(2):
-            new_xg(i)
-            new_xc(i)
-        copy_quant_recv_by_pass(0)
+        widen_share(0, nc.vector.tensor_copy)
+        turn_recv(0)
+        turn_share(0)
+        new_x(0)
+        new_x(1)
+        for g in range(PASSES):
+            nc.vector.tensor_copy(
+                out=x[0][:, K_PASS * g : K_PASS * (g + 1)].bitcast(F32).rearrange("p (r u) -> p r u", u=2),
+                in_=turned[RECV, 0][:].rearrange("p (u g) r -> p g r u", u=2)[:, g],
+            )
+        for g in range(PASSES):
+            quantise_x(0, K_PASS * g, K_PASS * (g + 1))
         scale_share(0)
-        if CFG["shr"] and CFG["sh1"]:
-            shuffle_recv(1)
-        if cv < 2:
-            cast_share(1, False)
-        if CFG["shr"] and CFG["sh2e"]:
-            shuffle_recv(2)
-        new_up(0)
+        widen_share(1, nc.scalar.copy)
+        new_u(0)
         for g in range(PASSES):
             for h in range(2):
-                mm_up_pass(0, h, 0, g)
-        transpose_recv(1)
-        transpose_share(1)
-        copy_recv(1, on_vector=CFG["cv1"])
-        quant_x(0, 1, 2)
+                multiply_u(0, h, RECV, g)
+        quantise_x(0, D, 2 * D)
+        turn_recv(1)
+        turn_share(1)
+        interleave(nc.scalar.copy, (RECV, 1), x[1][:, 0:D])
         scale_share(1)
         for g in range(PASSES):
             for h in range(2):
-                mm_up_pass(0, h, 1, g)
-        if CFG["shr"] and not CFG["sh2e"]:
-            shuffle_recv(2)
-        cast_share(2, cv >= 3)
-        quant_x(1, 0, 2)
-        spread_gain()
+                multiply_u(0, h, SHARE, g)
+        widen_share(2, nc.scalar.copy)
+        quantise_x(1, 0, 2 * D)
         silu(0, 0)
         silu(0, 1)
-        gain(0)
+
+        adds = []
         for i in range(1, TILES + 1):
-            h_now = [] if i == 1 else [i - 2] if i < CFG["cu"] else [i - 2, i - 1] if i == CFG["cu"] else [i - 1]
-            if i == 1:
-                out_now = []
-            elif i < CFG["cu"]:
-                out_now = [(i - 2, 0), (i - 2, 1)]
-            elif i == CFG["cu"]:
-                out_now = [(i - 2, 0), (i - 2, 1), (i - 1, 0)]
-            elif i == TILES:
-                out_now = [(i - 2, 1), (i - 1, 0), (i - 1, 1)]
-            else:
-                out_now = [(i - 2, 1), (i - 1, 0)]
-            xn = i + 1 if i + 1 < TILES else None
-            xs = i + 2 if i + 2 < TILES else None
-            for j in h_now[:-1]:
-                transpose_words(hs[j][:], True, ("h", j))
-            if xn is not None:
-                transpose_recv(xn)
-                transpose_share(xn)
-                new_xg(xn)
-                new_xc(xn)
-            for j in h_now[:-1]:
-                copy_h(j)
-                quant_h(j)
-            if xn is not None:
-                copy_recv(xn)
-            for j in h_now[-1:]:
-                transpose_words(hs[j][:], True, ("h", j))
-                copy_h(j)
-            if xs is not None:
-                if CFG["cfirst"]:
-                    cast_share(xs)
-                if CFG["shr"]:
-                    shuffle_recv(xs)
-                if not CFG["cfirst"]:
-                    cast_share(xs)
-                if CFG["shs"]:
-                    shuffle_share(xs)
-            if xn is not None:
-                scale_share(xn)
-            if CFG["addpos"] == 0 and 3 <= i < TILES:
-                add_store(i - 3)
-            for j in h_now[-1:]:
-                quant_h(j)
             if i == TILES:
-                add_store(i - 3, HALF, D)
-            if CFG["addpos"] == 1 and 3 <= i < TILES:
-                add_store(i - 3)
-            if xn is not None:
-                quant_x(xn, 0, 2)
+                hidden_tiles = [LAST]
+                halves = [(LAST - 1, 1), (LAST, 0), (LAST, 1)]
+            elif i == LAST:
+                hidden_tiles = [LAST - 2, LAST - 1]
+                halves = [(LAST - 2, 0), (LAST - 2, 1), (LAST - 1, 0)]
+            elif i >= 2:
+                hidden_tiles = [i - 2]
+                halves = [(i - 2, 0), (i - 2, 1)]
+            else:
+                hidden_tiles = []
+                halves = []
+
+            if i + 1 < TILES:
+                turn_recv(i + 1)
+                turn_share(i + 1)
+                new_x(i + 1)
+                interleave(nc.scalar.copy, (RECV, i + 1), x[i + 1][:, 0:D])
+            if i == 1:
+                turn_gain()
+            for j in hidden_tiles:
+                turn(hidden[j][:], True, ("hidden", j))
+                interleave_hidden(j)
+            if i + 2 < TILES:
+                widen_share(i + 2, nc.scalar.copy)
+                ordered_recv[i + 2] = order_words(recv[i + 2], "ordered_recv")
+                ordered_share[i + 2] = order_words(share[i + 2][:], "ordered_share")
+            if i + 1 < TILES:
+                scale_share(i + 1)
+            if i == 1:
+                copy_gain()
+                apply_gain(0)
+            for j in hidden_tiles:
+                quantise_hidden(j)
+            for j, h in adds:
+                add_and_store(j, h, nc.vector, 1)
+            adds = []
+            if i + 1 < TILES:
+                quantise_x(i + 1, 0, 2 * D)
+
             if i < TILES:
-                new_up(i)
-                mm_up(i, 0)
-                silu(i, 0)
-                mm_up(i, 1)
-                silu(i, 1)
-                if i == TILES - 1:
-                    add_store(i - 2, 0, HALF)
-                gain(i)
-            for n, (j, h) in enumerate(out_now):
-                mm_out(j, "gate", h)
+                new_u(i)
+                for h in range(2):
+                    for operand in (RECV, SHARE):
+                        for g in range(PASSES):
+                            multiply_u(i, h, operand, g)
+                    silu(i, h)
+                apply_gain(i)
+
+            for j, h in halves:
+                multiply_out(j, GATE, h)
                 tanh(j, h)
-                mm_out(j, "delta", h)
-                gate_delta(j, h)
-                if i == TILES and n == 1:
-                    add_store(j - 1)
-                if i == TILES - 1 and n == 1:
-                    pass
-        add_store(TILES - 1, 0, HALF)
-        add_store(TILES - 1, HALF, D)
+                multiply_out(j, DELTA, h)
+                if (j, h) == (LAST, 1):
+                    add_and_store(j, 0, nc.vector, 1)
+                    gate_delta(j, h, 2)
+                    add_and_store(j, h, nc.vector, 2)
+                else:
+                    gate_delta(j, h, 1)
+                    if (j, h) == (LAST, 0):
+                        for a in adds:
+                            add_and_store(a[0], a[1], nc.vector, 1)
+                    elif h == 1:
+                        add_and_store(j, h, nc.gpsimd, 1)
+                    else:
+                        adds.append((j, h))

@@ -117,9 +117,9 @@ def tile_cachetocachegatedkeyfuser_w4_kernel(
         load_recv(1, 1)
         load_words(SHARE, w_share_words)
         load_scales(SHARE, w_share_scales)
-        load_gain()
         load_share(2, 2)
         load_recv(2, 1)
+        load_gain()
         load_recv(3, 1)
         load_words(GATE, w_gate_words)
         load_scales(GATE, w_gate_scales)
@@ -414,7 +414,7 @@ def tile_cachetocachegatedkeyfuser_w4_kernel(
                     if (j, h) == (LAST, 0):
                         for a in adds:
                             add_and_store(a[0], a[1], nc.vector, 1)
-                    elif h == 1:
+                    elif h == 0 or j == LAST - 1:
                         add_and_store(j, h, nc.gpsimd, 1)
                     else:
                         adds.append((j, h))

from contextlib import ExitStack

import concourse.mybir as mybir
from concourse.masks import make_identity

T, D, F = 1024, 1024, 1024
FLOPS = 4 * 2 * T * D * F

F32 = mybir.dt.float32
BF16 = mybir.dt.bfloat16
U32 = mybir.dt.uint32
I32 = mybir.dt.int32
U8 = mybir.dt.uint8
FP8 = mybir.dt.float8_e4m3fn
FP8X4 = mybir.dt.float8_e4m3fn_x4
FP4X4 = mybir.dt.float4_e2m1fn_x4
ACT = mybir.ActivationFunctionType
ALU = mybir.AluOpType

P = 128
TILES = T // P
LAST = TILES - 1
K_PASS = 512
PASSES = D // K_PASS
HALF = 512
RECV, SHARE = 0, 1
GATE, DELTA = "gate", "delta"
WARM_UP = 4
ORDERED_FROM = 3


def tile_cachetocachegatedkeyfuser_w4_kernel(
    tc,
    k_recv,
    k_share_bytes,
    k_share_scale,
    w_recv_words,
    w_recv_scales,
    w_share_words,
    w_share_scales,
    g_hid,
    w_delta_words,
    w_delta_scales,
    w_gate_words,
    w_gate_scales,
    out,
):
    nc = tc.nc

    with ExitStack() as ctx:
        keep = ctx.enter_context(tc.tile_pool(name="keep", bufs=1))
        work = ctx.enter_context(tc.tile_pool(name="work", bufs=3))
        psum = ctx.enter_context(tc.psum_pool(name="psum", bufs=1))
        ctx.enter_context(tc.manual_schedule())

        zeros = keep.tile([P, HALF], BF16, name="zeros", align_bytes=64)
        nc.gpsimd.memset(zeros[:], 0.0)
        ident = keep.tile([P, P], F32, name="ident", align_bytes=64)
        make_identity(nc, ident[:])

        first = keep.tile([P, 1], F32, name="first")
        nc.vector.memset(first[:], 0.0)
        nc.scalar.activation(out=first[:], in_=first[:], func=ACT.Silu)

        words = {}
        scales = {}
        for name in (RECV, SHARE, GATE, DELTA):
            words[name] = keep.tile([P, PASSES, 2 * F], U8, name="words_%s" % name, align_bytes=256)
            scales[name] = keep.tile([P, PASSES, F], U8, name="scales_%s" % name, align_bytes=256)
            nc.vector.memset(scales[name][:].rearrange("p g n -> p (g n)").bitcast(I32), 0)

        def load_words(name, w_words):
            nc.sync.dma_start(out=words[name][:].bitcast(I32), in_=w_words.bitcast(I32).rearrange("g p n -> p g n"))

        def load_scales(name, w_scales):
            rows = w_scales.bitcast(I32).rearrange("g q n -> q g n")
            for q in range(4):
                nc.sync.dma_start(
                    out=scales[name][32 * q : 32 * q + 4, :, :].bitcast(I32), in_=rows[4 * q : 4 * q + 4, :, :]
                )

        recv = {}
        share_bytes = {}

        def load_recv(i, count):
            t = keep.tile([P, count, D], BF16, name="recv_%d" % i, align_bytes=64)
            nc.sync.dma_start(out=t[:], in_=k_recv[i * P : (i + count) * P, :].rearrange("(n p) d -> p n d", p=P))
            for n in range(count):
                recv[i + n] = t[:, n, :]

        def load_share(i, count):
            t = keep.tile([P, count, D], U8, name="share_bytes_%d" % i, align_bytes=64)
            nc.sync.dma_start(
                out=t[:], in_=k_share_bytes[i * P : (i + count) * P, :].rearrange("(n p) d -> p n d", p=P)
            )
            for n in range(count):
                share_bytes[i + n] = t[:, n, :]

        share_scale = keep.tile([P, 4 * PASSES], F32, name="share_scale")

        def load_share_scale():
            nc.sync.dma_start(
                out=share_scale[:].rearrange("p (g t) -> p g t", t=4),
                in_=k_share_scale.rearrange("o (g p t) -> p (o g) t", p=P, t=4),
            )

        gain_rows = keep.tile([P, 8], BF16, name="gain_rows")

        def load_gain():
            nc.sync.dma_start(out=gain_rows[:], in_=g_hid.rearrange("(n m) -> n m", m=8))

        load_recv(0, 1)
        load_share(0, 2)
        load_share_scale()
        load_scales(RECV, w_recv_scales)
        load_words(RECV, w_recv_words)
        load_recv(1, 1)
        load_words(SHARE, w_share_words)
        load_scales(SHARE, w_share_scales)
        load_share(2, 2)
        load_recv(2, 1)
        load_gain()
        load_recv(3, 1)
        load_words(GATE, w_gate_words)
        load_scales(GATE, w_gate_scales)
        load_share(4, 4)
        load_recv(4, 2)
        load_words(DELTA, w_delta_words)
        load_scales(DELTA, w_delta_scales)
        load_recv(6, 2)

        ordered_recv = {}
        ordered_share = {}
        share = {}
        turned = {}

        def widen_share(i, engine_copy):
            share[i] = work.tile([P, D], BF16, name="share", align_bytes=64)
            engine_copy(out=share[i][:], in_=share_bytes[i].bitcast(FP8))

        def order_words(src, name):
            t = work.tile([P, D], BF16, name=name, align_bytes=64)
            nc.scalar.copy(
                out=t[:].bitcast(F32).rearrange("p (g u m) -> p g u m", g=PASSES, u=2),
                in_=src.bitcast(F32).rearrange("p (g m u) -> p g u m", g=PASSES, u=2),
            )
            return t

        def turn(src, ordered, key):
            bank = psum.tile([P, 4, P], F32, name="turned", bufs=3)
            w = src.bitcast(F32)
            for g in range(PASSES):
                for u in range(2):
                    if ordered:
                        block = w[:, (2 * g + u) * P : (2 * g + u + 1) * P]
                    else:
                        block = w[:, 2 * P * g + u : 2 * P * (g + 1) : 2]
                    nc.tensor.transpose(bank[:, 2 * u + g, :], block, ident[:])
            turned[key] = bank

        def turn_recv(i):
            if i >= ORDERED_FROM:
                turn(ordered_recv[i][:], True, (RECV, i))
            else:
                turn(recv[i], False, (RECV, i))

        def turn_share(i):
            if i >= ORDERED_FROM:
                turn(ordered_share[i][:], True, (SHARE, i))
            else:
                turn(share[i][:], False, (SHARE, i))

        def interleave(engine_copy, key, dst):
            engine_copy(
                out=dst.bitcast(F32).rearrange("p (x u) -> p x u", u=2),
                in_=turned[key][:].rearrange("p (u g) r -> p (g r) u", u=2),
            )

        x = {}
        x_codes = {}
        x_scales = {}

        def new_x(i):
            x[i] = work.tile([P, 2 * D], BF16, name="x", align_bytes=64)
            x_codes[i] = work.tile([P, 2 * D // 4], U32, name="x_codes", align_bytes=64)
            x_scales[i] = work.tile([P, 2 * D // 4], U8, name="x_scales", align_bytes=64)

        def quantise_x(i, start, stop):
            c = slice(start // 4, stop // 4)
            nc.vector.quantize_mx(
                out=x_codes[i][:, c].bitcast(FP8X4), scales=x_scales[i][:, c], in_=x[i][:, start:stop]
            )

        def scale_share(i):
            v = turned[SHARE, i][:].rearrange("p a r -> p (a r)").bitcast(BF16)
            s = share_scale[:].rearrange("p (g u e) -> p g u e", u=2, e=2)
            nc.vector.tensor_tensor(
                out=x[i][:, D : 2 * D].rearrange("p (g r u e) -> p g r u e", g=PASSES, u=2, e=2),
                in0=v.rearrange("p (u g r e) -> p g r u e", u=2, g=PASSES, e=2),
                in1=s.unsqueeze(2).to_broadcast([P, PASSES, P, 2, 2]),
                op=ALU.mult,
            )

        u_bank = {}

        def new_u(i):
            for h in range(2):
                u_bank[i, h] = psum.tile([P, HALF], F32, name="sums", bufs=5)

        def multiply_u(i, h, operand, g):
            c = slice((operand * PASSES + g) * P, (operand * PASSES + g + 1) * P)
            nc.tensor.matmul_mx(
                out=u_bank[i, h][:],
                lhsT=x_codes[i][:, c].bitcast(FP8X4),
                lhsT_scale=x_scales[i][:, c],
                rhs=words[operand][:, g, 2 * HALF * h : 2 * HALF * (h + 1)].bitcast(FP4X4),
                rhs_scale=scales[operand][:, g, HALF * h : HALF * (h + 1)],
                start=(operand == RECV and g == 0),
                stop=(operand == SHARE and g == PASSES - 1),
            )

        silu_u = {}
        hidden = {}
        half_gain = keep.tile([P, F], BF16, name="half_gain", align_bytes=64)

        def silu(i, h):
            if h == 0:
                silu_u[i] = work.tile([P, F], F32, name="silu_u", align_bytes=64)
            nc.scalar.activation(
                out=silu_u[i][:, HALF * h : HALF * (h + 1)].rearrange("p (u m e) -> p u m e", u=2, e=2),
                in_=u_bank[i, h][:].rearrange("p (m u e) -> p u m e", u=2, e=2),
                func=ACT.Silu,
            )

        def apply_gain(i):
            hidden[i] = work.tile([P, F], BF16, name="hidden", bufs=4, align_bytes=64)
            nc.vector.tensor_tensor(out=hidden[i][:], in0=silu_u[i][:], in1=half_gain[:], op=ALU.mult)

        def turn_gain():
            rows = half_gain_rows[:].bitcast(F32)
            bank = psum.tile([P, 4, P], F32, name="turned", bufs=3)
            for w in range(4):
                nc.tensor.transpose(bank[:, w, :], rows[:, w : w + 1].to_broadcast([P, P]), ident[:])
            turned["gain"] = bank

        def copy_gain():
            rows_of_pass = P // PASSES
            for g in range(PASSES):
                nc.vector.tensor_copy(
                    out=half_gain[:, HALF * g : HALF * (g + 1)]
                    .bitcast(F32)
                    .rearrange("p (u n a) -> p u n a", u=2, a=2),
                    in_=turned["gain"][:, :, rows_of_pass * g : rows_of_pass * (g + 1)].rearrange(
                        "p (a u) n -> p u n a", u=2
                    ),
                )

        y = {}
        y_codes = {}
        y_scales = {}

        def interleave_hidden(j):
            y[j] = work.tile([P, F], BF16, name="y", align_bytes=64)
            interleave(nc.scalar.copy, ("hidden", j), y[j][:])

        def quantise_hidden(j):
            y_codes[j] = work.tile([P, F // 4], U32, name="y_codes", align_bytes=64)
            y_scales[j] = work.tile([P, F // 4], U8, name="y_scales", align_bytes=64)
            nc.vector.quantize_mx(out=y_codes[j][:].bitcast(FP8X4), scales=y_scales[j][:], in_=y[j][:])

        o_bank = {}
        tanh_v = {}
        update = {}

        def multiply_out(j, name, h):
            bank = psum.tile([P, HALF], F32, name="sums", bufs=5)
            for g in range(PASSES):
                c = slice(P * g, P * (g + 1))
                nc.tensor.matmul_mx(
                    out=bank[:],
                    lhsT=y_codes[j][:, c].bitcast(FP8X4),
                    lhsT_scale=y_scales[j][:, c],
                    rhs=words[name][:, g, 2 * HALF * h : 2 * HALF * (h + 1)].bitcast(FP4X4),
                    rhs_scale=scales[name][:, g, HALF * h : HALF * (h + 1)],
                    start=(g == 0),
                    stop=(g == PASSES - 1),
                )
            o_bank[j, name, h] = bank

        def tanh(j, h):
            tanh_v[j, h] = work.tile([P, HALF], F32, name="tanh_v", align_bytes=64)
            nc.scalar.activation(out=tanh_v[j, h][:], in_=o_bank[j, GATE, h][:], func=ACT.Tanh)

        def gate_delta(j, h, parts):
            update[j, h] = work.tile([P, HALF], F32, name="update", bufs=6, align_bytes=64)
            for n in range(parts):
                c = slice(HALF // parts * n, HALF // parts * (n + 1))
                nc.vector.scalar_tensor_tensor(
                    out=update[j, h][:, c],
                    in0=tanh_v[j, h][:, c],
                    scalar=1.0,
                    in1=o_bank[j, DELTA, h][:, c],
                    op0=ALU.add,
                    op1=ALU.mult,
                )

        def add_and_store(j, h, engine, parts):
            result = work.tile([P, HALF], F32, name="result", bufs=6, align_bytes=64)
            for n in range(parts):
                c = slice(HALF // parts * n, HALF // parts * (n + 1))
                d = slice(HALF * h + HALF // parts * n, HALF * h + HALF // parts * (n + 1))
                engine.tensor_tensor(out=result[:, c], in0=update[j, h][:, c], in1=recv[j][:, d], op=ALU.add)
                nc.sync.dma_start(out=out[j * P : (j + 1) * P, d], in_=result[:, c])

        half_gain_rows = keep.tile([P, 8], BF16, name="half_gain_rows")
        nc.gpsimd.tensor_scalar(out=half_gain_rows[:], in0=gain_rows[:], scalar1=0.5, scalar2=None, op0=ALU.mult)

        warm_bank = psum.tile([P, HALF], F32, name="sums", bufs=5)
        for n in range(WARM_UP):
            nc.tensor.matmul(warm_bank[:], lhsT=zeros[:, 0:P], rhs=zeros[:], start=True, stop=True)

        widen_share(0, nc.vector.tensor_copy)
        turn_recv(0)
        turn_share(0)
        new_x(0)
        new_x(1)
        for g in range(PASSES):
            nc.vector.tensor_copy(
                out=x[0][:, K_PASS * g : K_PASS * (g + 1)].bitcast(F32).rearrange("p (r u) -> p r u", u=2),
                in_=turned[RECV, 0][:].rearrange("p (u g) r -> p g r u", u=2)[:, g],
            )
        for g in range(PASSES):
            quantise_x(0, K_PASS * g, K_PASS * (g + 1))
        scale_share(0)
        widen_share(1, nc.scalar.copy)
        new_u(0)
        for g in range(PASSES):
            for h in range(2):
                multiply_u(0, h, RECV, g)
        quantise_x(0, D, 2 * D)
        turn_recv(1)
        turn_share(1)
        interleave(nc.scalar.copy, (RECV, 1), x[1][:, 0:D])
        scale_share(1)
        for g in range(PASSES):
            for h in range(2):
                multiply_u(0, h, SHARE, g)
        widen_share(2, nc.scalar.copy)
        quantise_x(1, 0, 2 * D)
        silu(0, 0)
        silu(0, 1)

        adds = []
        for i in range(1, TILES + 1):
            if i == TILES:
                hidden_tiles = [LAST]
                halves = [(LAST - 1, 1), (LAST, 0), (LAST, 1)]
            elif i == LAST:
                hidden_tiles = [LAST - 2, LAST - 1]
                halves = [(LAST - 2, 0), (LAST - 2, 1), (LAST - 1, 0)]
            elif i >= 2:
                hidden_tiles = [i - 2]
                halves = [(i - 2, 0), (i - 2, 1)]
            else:
                hidden_tiles = []
                halves = []

            if i + 1 < TILES:
                turn_recv(i + 1)
                turn_share(i + 1)
                new_x(i + 1)
                interleave(nc.scalar.copy, (RECV, i + 1), x[i + 1][:, 0:D])
            if i == 1:
                turn_gain()
            for j in hidden_tiles:
                turn(hidden[j][:], True, ("hidden", j))
                interleave_hidden(j)
            if i + 2 < TILES:
                widen_share(i + 2, nc.scalar.copy)
                ordered_recv[i + 2] = order_words(recv[i + 2], "ordered_recv")
                ordered_share[i + 2] = order_words(share[i + 2][:], "ordered_share")
            if i + 1 < TILES:
                scale_share(i + 1)
            if i == 1:
                copy_gain()
                apply_gain(0)
            for j in hidden_tiles:
                quantise_hidden(j)
            for j, h in adds:
                add_and_store(j, h, nc.vector, 1)
            adds = []
            if i + 1 < TILES:
                quantise_x(i + 1, 0, 2 * D)

            if i < TILES:
                new_u(i)
                for h in range(2):
                    for operand in (RECV, SHARE):
                        for g in range(PASSES):
                            multiply_u(i, h, operand, g)
                    silu(i, h)
                apply_gain(i)

            for j, h in halves:
                multiply_out(j, GATE, h)
                tanh(j, h)
                multiply_out(j, DELTA, h)
                if (j, h) == (LAST, 1):
                    add_and_store(j, 0, nc.vector, 1)
                    gate_delta(j, h, 2)
                    add_and_store(j, h, nc.vector, 2)
                else:
                    gate_delta(j, h, 1)
                    if (j, h) == (LAST, 0):
                        for a in adds:
                            add_and_store(a[0], a[1], nc.vector, 1)
                    elif h == 0 or j == LAST - 1:
                        add_and_store(j, h, nc.gpsimd, 1)
                    else:
                        adds.append((j, h))
